import numpy as np
import ml_dtypes


def mxq(x, axis, fmt="e4m3"):
    dtype, down = {"e4m3": (ml_dtypes.float8_e4m3fn, 7), "e5m2": (ml_dtypes.float8_e5m2, 14)}[fmt]
    v = np.moveaxis(np.asarray(x, np.float32).astype(ml_dtypes.bfloat16).astype(np.float64), axis, -1)
    blocks = v.reshape(v.shape[:-1] + (-1, 32))
    amax = np.abs(blocks).max(-1, keepdims=True)
    byte = np.maximum(np.where(amax > 0, np.frexp(amax)[1] - 1 + 127, 0) - down, 1)
    scale = np.exp2(byte - 127.0)
    codes = (blocks / scale).astype(np.float32).astype(dtype).astype(np.float64)
    return np.moveaxis((codes * scale).reshape(v.shape), -1, axis)


WIDE = False


def mx_kscale(k):
    if not WIDE:
        return np.ones(k)
    levels = np.array([10, -10, 5, -5, 0])
    if k % 512:
        return np.exp2(np.random.permutation(np.resize(levels, k // 32))).repeat(32)
    a = np.empty((k // 512, 16))
    for p in range(k // 512):
        a[p, :8] = np.random.permutation(np.resize(levels, 8))
        for g in range(8):
            far = levels[np.abs(levels - a[p, g]) >= 10]
            a[p, g + 8] = far[np.random.randint(len(far))]
    return np.exp2(a.ravel()).repeat(32)


BF16 = ml_dtypes.bfloat16


def bf(x):
    return np.asarray(x, np.float32).astype(BF16)


def f64(x):
    return np.asarray(x).astype(np.float64)


E2M1 = np.array([0.0, 0.5, 1.0, 1.5, 2.0, 3.0, 4.0, 6.0, -0.0, -0.5, -1.0, -1.5, -2.0, -3.0, -4.0, -6.0])


def pack_weight(w, fmt):
    k, n = w.shape
    w = f64(bf(w)).reshape(k // 32, 32, n)
    amax = np.abs(w).max(1)
    if fmt == "e4m3":
        byte = np.frexp(amax)[1] - 1 + 127 - 7
    else:
        mant, ex = np.frexp(amax / 6.0)
        byte = np.where(mant > 0.5, ex, ex - 1) + 127
    byte = np.clip(np.where(amax > 0, byte, 1), 1, 254)
    scaled = (w * np.exp2(127.0 - byte)[:, None, :]).reshape(k, n).astype(np.float32)
    by_word = np.ascontiguousarray(scaled.reshape(k // 512, 128, 4, n).transpose(0, 1, 3, 2))
    if fmt == "e4m3":
        words = by_word.astype(ml_dtypes.float8_e4m3fn).view(np.uint8)
    else:
        c = by_word.astype(ml_dtypes.float4_e2m1fn).view(np.uint8) & 0xF
        words = c[..., 0::2] | (c[..., 1::2] << 4)
    return np.ascontiguousarray(words), np.ascontiguousarray(byte.astype(np.uint8).reshape(k // 512, 16, n))


def unpack_weight(words, scales, fmt):
    g, p, n, _ = words.shape
    if fmt == "e4m3":
        vals = np.ascontiguousarray(words).view(ml_dtypes.float8_e4m3fn).astype(np.float64)
    else:
        nib = np.empty((g, p, n, 4), np.uint8)
        nib[..., 0::2] = words & 0xF
        nib[..., 1::2] = words >> 4
        vals = E2M1[nib]
    vals = vals * np.repeat(np.exp2(scales.astype(np.float64) - 127.0), 8, axis=1)[..., None]
    return vals.transpose(0, 1, 3, 2).reshape(g * 512, n)
def pack4(w):
    words, scales = pack_weight(w, "e2m1")
    return words.reshape(words.shape[0], 128, -1), scales


def unpack4(words, scales):
    return unpack_weight(words.reshape(words.shape[0], 128, -1, 2), scales, "e2m1")


E4M3FN = np.array([(-1.0 if i & 128 else 1.0) * ((1.0 + (i & 7) / 8.0) * 2.0 ** (((i >> 3) & 15) - 7) if i & 120 else (i & 7) * 2.0 ** -9) for i in range(256)])


def e4m3fn_bytes(y):
    return np.clip(np.asarray(y, np.float64), -448.0, 448.0).astype(np.float32).astype(ml_dtypes.float8_e4m3fn).view(np.uint8)


def e4m3fn_values(b):
    return E4M3FN[b]

def planes(Y):
    n, m = Y.shape
    b = f64(bf(Y)).reshape(n // 32, 32, m)
    amax = np.abs(b).max(1)
    byte = np.clip(np.where(amax > 0, np.frexp(amax)[1] - 1 + 127 - 7, 1), 1, 254)
    codes = (b * np.exp2(127.0 - byte)[:, None, :]).reshape(n, m).astype(np.float32).astype(ml_dtypes.float8_e4m3fn).view(np.uint8)
    words = codes.reshape(n // 512, 128, 4, m).transpose(0, 1, 3, 2)
    return np.ascontiguousarray(words), np.ascontiguousarray(byte.astype(np.uint8).reshape(n // 512, 16, m))


G, T, KV, KQ, F, A, B = 4, 256, 2048, 512, 1024, 1024, 128
E4M3_MAX = 448.0

def setup_inputs():
    rn = np.random.randn
    sv, sq, t = mx_kscale(KV), mx_kscale(KQ), mx_kscale(F)
    V = rn(G, T, KV) * np.exp(0.3 * rn(G, T, 1)) * sv
    Q = rn(G, T, KQ) * np.exp(0.3 * rn(G, T, 1)) * sq
    U = rn(G, KV, F) / np.sqrt(KV) / sv[:, None]
    W = 1.5 * rn(G, KQ, F) / np.sqrt(KQ) / sq[:, None] * t
    R = rn(G, KQ, A) / np.sqrt(KQ) / sq[:, None]
    C = rn(G, F, A) / np.sqrt(F) / t[:, None] * np.exp(0.8 * rn(G, 1, A))
    V_scale = np.float32(np.abs(V).reshape(G, T, KV // B, B).max(axis=3) / E4M3_MAX)
    Q_scale = np.float32(np.abs(Q).reshape(G, T, KQ // B, B).max(axis=3) / E4M3_MAX)
    V_bytes = e4m3fn_bytes(V / np.repeat(f64(V_scale), B, axis=2))
    Q_bytes = e4m3fn_bytes(Q / np.repeat(f64(Q_scale), B, axis=2))
    U_words, U_scales = pack4(U.reshape(G * KV, F))
    W_words, W_scales = pack4(W.reshape(G * KQ, F))
    R_words, R_scales = pack4(R.reshape(G * KQ, A))
    C_words, C_scales = pack4(C.reshape(G * F, A))
    return {"V_bytes": V_bytes, "V_scale": V_scale, "Q_bytes": Q_bytes, "Q_scale": Q_scale,
            "U_words": U_words, "U_scales": U_scales, "W_words": W_words, "W_scales": W_scales,
            "R_words": R_words, "R_scales": R_scales, "C_words": C_words, "C_scales": C_scales,
            "c": bf(0.4 * rn(G, A))}

def reference(V_bytes, V_scale, Q_bytes, Q_scale, U_words, U_scales, W_words, W_scales, R_words, R_scales, C_words, C_scales, c):
    V = e4m3fn_values(V_bytes) * np.repeat(f64(V_scale), B, axis=2)
    Q = e4m3fn_values(Q_bytes) * np.repeat(f64(Q_scale), B, axis=2)
    U = unpack4(U_words, U_scales).reshape(G, KV, F)
    W = unpack4(W_words, W_scales).reshape(G, KQ, F)
    R = unpack4(R_words, R_scales).reshape(G, KQ, A)
    C = unpack4(C_words, C_scales).reshape(G, F, A)
    Vq = mxq(V, 2, "e4m3")
    Qq = mxq(Q, 2, "e4m3")
    a = Vq @ U
    b = Qq @ W
    r = Qq @ R
    h = np.tanh(a) * b
    hq = mxq(h, 2, "e4m3")
    z = hq @ C
    y = (z + f64(c).reshape(G, 1, A)) * (1.0 / (1.0 + np.exp(-r)))
    Y = y.reshape(G * T, A).T
    words, scales = planes(Y)
    return y, words, scales

@@ -1,0 +1,502 @@
+from contextlib import ExitStack
+
+import concourse.mybir as mybir
+from concourse.masks import make_identity
+
+G, T, KV, KQ, F, A = 4, 256, 2048, 512, 1024, 1024
+FLOPS = 2 * G * T * (KV * F + KQ * F + KQ * A + F * A)
+
+F32 = mybir.dt.float32
+BF16 = mybir.dt.bfloat16
+I32 = mybir.dt.int32
+U32 = mybir.dt.uint32
+U8 = mybir.dt.uint8
+FP8 = mybir.dt.float8_e4m3fn
+FP8X4 = mybir.dt.float8_e4m3fn_x4
+FP4X4 = mybir.dt.float4_e2m1fn_x4
+ACT = mybir.ActivationFunctionType
+ALU = mybir.AluOpType
+
+P = 128
+KP = 512
+N = 512
+BLK = 128
+TILES = G * T // P
+BANKS = 8
+
+
+def tile_grouped_vqa_fusion_b12_kernel(tc, V_bytes, V_scale, Q_bytes, Q_scale, U_words, U_scales,
+                                                   W_words, W_scales, R_words, R_scales, C_words, C_scales, c,
+                                                   out_0, out_1, out_2):
+    nc = tc.nc
+    with ExitStack() as ctx:
+        keep = ctx.enter_context(tc.tile_pool(name="keep", bufs=1))
+        work = ctx.enter_context(tc.tile_pool(name="work", bufs=2))
+        psum = ctx.enter_context(tc.psum_pool(name="psum", bufs=1))
+        ctx.enter_context(tc.manual_schedule())
+
+        st = {}
+        taken = []
+
+        def bank():
+            n = len(taken) % BANKS
+            taken.append(n)
+            return psum.tile([P, N], F32, name="bank%d" % n, tag="bank%d" % n)
+
+        def wtile(shape, dtype, tag, bufs):
+            return work.tile(shape, dtype, name=tag, tag=tag, bufs=bufs, align_bytes=64)
+
+        def ktile(shape, dtype, tag):
+            return keep.tile(shape, dtype, name=tag, tag=tag, align_bytes=64)
+
+        weights = {"U": (U_words, U_scales, 4), "W": (W_words, W_scales, 1),
+                   "R": (R_words, R_scales, 1), "C": (C_words, C_scales, 2)}
+
+        ident = ktile([P, P], F32, "ident")
+        make_identity(nc, ident[:])
+
+        def clear_plane(w, slot):
+            plane = ktile([P, weights[w][2] * F], U8, "%s_plane%d" % (w, slot))
+            nc.vector.memset(plane[:].bitcast(I32), 0)
+            st[w, "plane", slot] = plane
+
+        for w in ("R", "U", "W", "C"):
+            clear_plane(w, 0)
+
+        last = TILES - 1
+        early = TILES - 2
+        y_scales_early = ktile([P, 2 * early * P], U8, "y_scales_early")
+        y_scales_last = ktile([P, 2 * 2 * P], U8, "y_scales_last")
+
+        def y_scales(i, j):
+            if i < early:
+                return y_scales_early[:, (j * early + i) * P:(j * early + i + 1) * P]
+            return y_scales_last[:, (2 * j + i - early) * P:(2 * j + i - early + 1) * P]
+
+        def load_v(i):
+            t = ktile([P, KV], U8, "v_bytes%d" % i)
+            nc.sync.dma_start(out=t[:], in_=V_bytes[i // 2, (i % 2) * P:(i % 2 + 1) * P, :])
+            st["vb", i] = t
+
+        def load_q(e):
+            t = ktile([P, 4 * KQ], U8, "q_bytes%d" % e)
+            nc.sync.dma_start(out=t[:].rearrange("p (i k) -> p i k", i=4),
+                              in_=Q_bytes.rearrange("e (h p) k -> p (e h) k", p=P)[:, 4 * e:4 * e + 4, :])
+            st["qb", e] = t
+
+        def load_act_scales(src, key, first, count):
+            nb = src.shape[2]
+            t = ktile([P, count * nb], F32, "%s%d" % (key, first))
+            nc.sync.dma_start(out=t[:].rearrange("p (i j) -> p i j", j=nb),
+                              in_=src.rearrange("e (h p) j -> p (e h) j", p=P)[:, first:first + count, :])
+            for i in range(count):
+                st[key, first + i] = (t, i * nb)
+
+        def load_words(w, e):
+            words, scales, passes = weights[w]
+            t = wtile([P, passes * 2 * F], U8, w + "_words", 2 if w == "U" else 3)
+            nc.sync.dma_start(out=t[:].bitcast(I32).rearrange("p (g n) -> p g n", g=passes),
+                              in_=words.bitcast(I32)[passes * e:passes * (e + 1)].rearrange("g p n -> p g n"))
+            for g in range(passes):
+                for j in range(2):
+                    st[w, "words", e, g, j] = t[:, 2 * (g * F + j * N):2 * (g * F + (j + 1) * N)]
+
+        def load_words_half(w, e, j):
+            words, scales, passes = weights[w]
+            t = ktile([P, passes * 2 * N], U8, "%s_words_half%d" % (w, j))
+            src = words.bitcast(I32)[passes * e:passes * (e + 1), :, j * N // 2:(j + 1) * N // 2]
+            nc.sync.dma_start(out=t[:].bitcast(I32).rearrange("p (g n) -> p g n", g=passes),
+                              in_=src.rearrange("g p n -> p g n"))
+            for g in range(passes):
+                st[w, "words", e, g, j] = t[:, 2 * g * N:2 * (g + 1) * N]
+
+        def load_planes(w, e):
+            words, scales, passes = weights[w]
+            plane = st[w, "plane", e % 2]
+            rows = scales.bitcast(I32).rearrange("g (q r) n -> r q g n", r=4)
+            for r in range(4):
+                nc.sync.dma_start(out=plane[r:P:32, :].bitcast(I32).rearrange("q (g n) -> q g n", g=passes),
+                                  in_=rows[r, :, passes * e:passes * (e + 1), :])
+
+        def load_c():
+            t = ktile([P, G * 8], BF16, "c_cols")
+            nc.sync.dma_start(out=t[:].rearrange("p (e j) -> p e j", e=G), in_=c.rearrange("e (p j) -> p e j", p=P))
+            st["c_cols"] = t
+
+        def live(i):
+            return 0 <= i < TILES
+
+        def widen(i, g):
+            if not live(i):
+                return
+            if g < 4:
+                src, base = st["vb", i], g * KP
+                sc, col = st["vs", i]
+                col = col + 4 * g
+            else:
+                src, base = st["qb", i // 4], (i % 4) * KQ
+                sc, col = st["qs", i]
+            wide = wtile([P, KP], BF16, "wide%d" % g, 2)
+            dst = wide[:].rearrange("t (u p e) -> t p u e", u=2, e=2)
+            for q in range(4):
+                blk = src[:, base + q * BLK:base + (q + 1) * BLK].bitcast(FP8)
+                nc.vector.tensor_scalar(out=dst[:, 32 * q:32 * (q + 1)],
+                                        in0=blk.rearrange("t (p u e) -> t p u e", u=2, e=2),
+                                        scalar1=sc[:, col + q:col + q + 1], scalar2=None, op0=ALU.mult)
+            st["wide", i, g] = wide
+
+        def turn(key, i, srcs):
+            if not live(i):
+                return
+            b = bank()
+            for j, k in enumerate(srcs):
+                words = st[k][:].bitcast(F32)
+                for u in range(2):
+                    nc.tensor.transpose(b[:, (2 * j + u) * P:(2 * j + u + 1) * P], words[:, u * P:(u + 1) * P], ident[:])
+            st["turned", key, i] = (b, len(srcs))
+
+        def empty(key, i):
+            if not live(i):
+                return
+            b, n = st["turned", key, i]
+            grouped = wtile([P, n * KP], BF16, "grouped_" + key, 2)
+            nc.scalar.copy(out=grouped[:].bitcast(F32).rearrange("p (j r u) -> p j r u", j=n, u=2),
+                           in_=b[:, 0:n * 2 * P].rearrange("p (j u r) -> p j r u", j=n, u=2))
+            st["grouped", key, i] = (grouped, n)
+
+        def quant(key, i):
+            if not live(i):
+                return
+            grouped, n = st["grouped", key, i]
+            codes = wtile([P, n * P], U32, "codes_" + key, 3)
+            scales = wtile([P, n * P], U8, "scales_" + key, 3)
+            nc.vector.quantize_mx(out=codes[:].bitcast(FP8X4), scales=scales[:], in_=grouped[:])
+            for j in range(n):
+                st["mx", key, i, j] = (codes[:, j * P:(j + 1) * P], scales[:, j * P:(j + 1) * P])
+
+        def product(name, w, i, j, acts, passes=None):
+            if not live(i):
+                return
+            e = i // 2
+            passes = range(len(acts)) if passes is None else passes
+            b = bank() if passes[0] == 0 else st[name, i, j]
+            plane = st[w, "plane", e % 2]
+            for g in passes:
+                codes, scales = st[acts[g]]
+                col = g * F + j * N
+                nc.tensor.matmul_mx(out=b[:], lhsT=codes.bitcast(FP8X4), lhsT_scale=scales,
+                                    rhs=st[w, "words", e, g, j].bitcast(FP4X4),
+                                    rhs_scale=plane[:, col:col + N],
+                                    start=(g == 0), stop=(g == len(acts) - 1))
+            st[name, i, j] = b
+
+        def v_acts(i):
+            return [("mx", "v0", i, 0), ("mx", "v0", i, 1), ("mx", "v1", i, 0), ("mx", "v1", i, 1)]
+
+        def paired(ap):
+            return ap.rearrange("t (p u e) -> t u p e", u=2, e=2)
+
+        def plain(ap):
+            return ap.rearrange("t (u p e) -> t u p e", u=2, e=2)
+
+        def sigmoid(i, j):
+            if not live(i):
+                return
+            s = wtile([P, N], F32, "mask%d" % j, 3)
+            nc.scalar.activation(out=s[:], in_=st["r", i, j][:], func=ACT.Sigmoid)
+            st["mask", i, j] = s
+
+        def tanh(i, j):
+            if not live(i):
+                return
+            t = wtile([P, N], F32, "tanh%d" % j, 2)
+            nc.scalar.activation(out=plain(t[:]), in_=paired(st["a", i, j][:]), func=ACT.Tanh)
+            st["tanh", i, j] = t
+
+        def joint(i, j):
+            if not live(i):
+                return
+            h = wtile([P, N], BF16, "joint%d" % j, 2)
+            nc.vector.tensor_tensor(out=plain(h[:]), in0=paired(st["b", i, j][:]), in1=plain(st["tanh", i, j][:]),
+                                    op=ALU.mult)
+            st["h", i, j] = h
+
+        def add_bias(i, j):
+            if not live(i):
+                return
+            t = wtile([P, N], F32, "biased%d" % j, 2)
+            nc.vector.tensor_tensor(out=t[:], in0=st["z", i, j][:], in1=st["c_rows", i // 2][:, j * N:(j + 1) * N],
+                                    op=ALU.add)
+            st["biased", i, j] = t
+
+        def apply_mask(i, j):
+            if not live(i):
+                return
+            y = wtile([P, N], F32, "y%d" % j, 3)
+            nc.vector.tensor_tensor(out=y[:], in0=st["biased", i, j][:], in1=st["mask", i, j][:], op=ALU.mult)
+            nc.sync.dma_start(out=out_0[i // 2, (i % 2) * P:(i % 2 + 1) * P, j * N:(j + 1) * N], in_=y[:])
+            st["y", i, j] = y
+
+        def round_y(i, j):
+            if not live(i):
+                return
+            yb = wtile([P, N], BF16, "y_bf%d" % j, 2)
+            nc.scalar.copy(out=plain(yb[:]), in_=paired(st["y", i, j][:]))
+            st["yb", i, j] = yb
+
+        def store_y_scales(plane, m0, width, queues):
+            rows = out_2.bitcast(I32).rearrange("g (q r) m -> r q g m", r=4)
+            for r in range(4):
+                queues[r % len(queues)].dma_start(out=rows[r, :, :, m0 // 4:(m0 + width) // 4],
+                                  in_=plane[r:P:32, :].bitcast(I32).rearrange("q (g m) -> q g m", g=2))
+
+        def mask_to_bf16(i, j):
+            yb = wtile([P, N], BF16, "y_bf%d" % j, 2)
+            nc.vector.tensor_tensor(out=plain(yb[:]), in0=paired(st["biased", i, j][:]),
+                                    in1=paired(st["mask", i, j][:]), op=ALU.mult)
+            st["yb", i, j] = yb
+
+        def quant_y_half(i, j):
+            grouped, n = st["grouped", "y%d" % j, i]
+            codes = wtile([P, P], U32, "y_codes_half", 2)
+            nc.vector.quantize_mx(out=codes[:].bitcast(FP8X4), scales=y_scales(i, j),
+                                  in_=grouped[:])
+            dst = out_1.rearrange("g p m t -> g p (m t)").bitcast(I32)
+            nc.sync.dma_start(out=dst[j, :, i * P:(i + 1) * P], in_=codes[:].bitcast(I32))
+
+        def quant_y(i):
+            if not live(i):
+                return
+            grouped, n = st["grouped", "y", i]
+            codes = wtile([P, 2 * P], U32, "y_codes", 4)
+            for j in range(2):
+                nc.vector.quantize_mx(out=codes[:, j * P:(j + 1) * P].bitcast(FP8X4), scales=y_scales(i, j),
+                                      in_=grouped[:, j * KP:(j + 1) * KP])
+            dst = out_1.rearrange("g p m t -> p g (m t)").bitcast(I32)
+            nc.sync.dma_start(out=dst[:, :, i * P:(i + 1) * P],
+                              in_=codes[:].bitcast(I32).rearrange("p (g m) -> p g m", g=2))
+            if i == early - 1:
+                store_y_scales(y_scales_early, 0, early * P, [nc.sync])
+
+        def spread_turn(e):
+            if not 0 <= e < G:
+                return
+            b = bank()
+            cols = st["c_cols"][:].bitcast(F32)
+            for j in range(4):
+                nc.tensor.transpose(b[:, j * P:(j + 1) * P],
+                                    cols[:, 4 * e + j:4 * e + j + 1].to_broadcast([P, P]), ident[:])
+            st["c_bank", e] = b
+
+        def spread_empty(e):
+            if not 0 <= e < G:
+                return
+            rows = ktile([P, A], BF16, "c_rows%d" % e)
+            nc.scalar.copy(out=rows[:].bitcast(F32).rearrange("t (p j) -> t p j", j=4),
+                           in_=st["c_bank", e][:].rearrange("t (j p) -> t p j", j=4))
+            st["c_rows", e] = rows
+
+        load_q(0)
+        load_act_scales(Q_scale, "qs", 0, 4)
+        load_v(0)
+        load_act_scales(V_scale, "vs", 0, 4)
+        load_v(1)
+        load_words("R", 0)
+        load_words_half("U", 0, 0)
+        load_planes("R", 0)
+        load_planes("U", 0)
+        load_words("W", 0)
+        load_v(2)
+        load_planes("W", 0)
+        load_words_half("U", 0, 1)
+        load_c()
+        load_v(3)
+        load_words("C", 0)
+        load_planes("C", 0)
+
+        def q_acts(i):
+            return [("mx", "q", i, 0)]
+
+        def h_acts(i):
+            return [("mx", "h", i, 0), ("mx", "h", i, 1)]
+
+        def turn_v(i, half):
+            turn("v%d" % half, i, [("wide", i, 2 * half), ("wide", i, 2 * half + 1)])
+
+        widen(0, 4)
+        turn("q", 0, [("wide", 0, 4)])
+        empty("q", 0)
+        for half in range(2):
+            widen(0, 2 * half)
+            widen(0, 2 * half + 1)
+            turn_v(0, half)
+            empty("v%d" % half, 0)
+        quant("q", 0)
+        quant("v0", 0)
+        product("r", "R", 0, 0, q_acts(0))
+        product("r", "R", 0, 1, q_acts(0))
+        widen(1, 4)
+        quant("v1", 0)
+        sigmoid(0, 0)
+        sigmoid(0, 1)
+        for g in range(4):
+            widen(1, g)
+        for w in ("U", "W", "R", "C"):
+            clear_plane(w, 1)
+        for w in ("U", "W", "R"):
+            load_words(w, 1)
+        for w in ("U", "W", "R"):
+            load_planes(w, 1)
+        load_v(4)
+        load_act_scales(V_scale, "vs", 4, 4)
+        load_q(1)
+        load_act_scales(Q_scale, "qs", 4, 4)
+        load_words("C", 1)
+        load_planes("C", 1)
+        load_v(5)
+        for w in ("U", "W", "R", "C"):
+            load_words(w, 2)
+        load_v(6)
+        load_v(7)
+        product("a", "U", 0, 0, v_acts(0))
+        product("b", "W", 0, 0, q_acts(0))
+        tanh(0, 0)
+        turn_v(1, 0)
+        turn_v(1, 1)
+        turn("q", 1, [("wide", 1, 4)])
+        empty("v0", 1)
+        widen(2, 0)
+        joint(0, 0)
+        product("a", "U", 0, 1, v_acts(0))
+        empty("v1", 1)
+        empty("q", 1)
+        product("b", "W", 0, 1, q_acts(0))
+        widen(2, 1)
+        quant("v0", 1)
+        tanh(0, 1)
+        quant("v1", 1)
+        widen(2, 2)
+        joint(0, 1)
+        quant("q", 1)
+        widen(2, 3)
+        widen(2, 4)
+
+        for s in range(1, last):
+            if s in (2, 4):
+                for w in ("U", "W", "R"):
+                    load_planes(w, s // 2 + 1)
+            if s in (3, 5):
+                load_planes("C", s // 2 + 1)
+            if s == 2:
+                for w in ("W", "R"):
+                    load_words(w, 3)
+            if s == 3:
+                load_words("C", 3)
+            if s == 4:
+                load_words("U", 3)
+            n, o = s + 1, s - 2
+            turn("h", s - 1, [("h", s - 1, 0), ("h", s - 1, 1)])
+            add_bias(o, 1)
+            turn_v(n, 0)
+            empty("h", s - 1)
+            turn_v(n, 1)
+            apply_mask(o, 0)
+            turn("q", n, [("wide", n, 4)])
+            turn("y", s - 3, [("yb", s - 3, 0), ("yb", s - 3, 1)])
+            empty("v0", n)
+            spread_turn(s - 1)
+            quant("h", s - 1)
+            widen(s + 2, 0)
+            empty("v1", n)
+            apply_mask(o, 1)
+            product("a", "U", s, 0, v_acts(s))
+            empty("q", n)
+            quant("v0", n)
+            quant("v1", n)
+            empty("y", s - 3)
+            spread_empty(s - 1)
+            product("b", "W", s, 0, q_acts(s))
+            tanh(s, 0)
+            widen(s + 2, 1)
+            quant_y(s - 3)
+            product("a", "U", s, 1, v_acts(s))
+            round_y(o, 0)
+            joint(s, 0)
+            product("b", "W", s, 1, q_acts(s))
+            quant("q", n)
+            widen(s + 2, 2)
+            tanh(s, 1)
+            product("r", "R", s, 0, q_acts(s))
+            widen(s + 2, 3)
+            product("r", "R", s, 1, q_acts(s))
+            round_y(o, 1)
+            joint(s, 1)
+            product("z", "C", s - 1, 0, h_acts(s - 1))
+            sigmoid(s, 0)
+            widen(s + 2, 4)
+            product("z", "C", s - 1, 1, h_acts(s - 1))
+            sigmoid(s, 1)
+            add_bias(s - 1, 0)
+
+        s = last
+        h_last = [("mx", "h0", s, 0), ("mx", "h1", s, 0)]
+        turn("h", s - 1, [("h", s - 1, 0), ("h", s - 1, 1)])
+        add_bias(s - 2, 1)
+        empty("h", s - 1)
+        apply_mask(s - 2, 0)
+        turn("y", s - 3, [("yb", s - 3, 0), ("yb", s - 3, 1)])
+        quant("h", s - 1)
+        apply_mask(s - 2, 1)
+        product("a", "U", s, 0, v_acts(s))
+        empty("y", s - 3)
+        round_y(s - 2, 0)
+        product("b", "W", s, 0, q_acts(s))
+        tanh(s, 0)
+        quant_y(s - 3)
+        product("a", "U", s, 1, v_acts(s))
+        round_y(s - 2, 1)
+        joint(s, 0)
+        product("b", "W", s, 1, q_acts(s))
+        tanh(s, 1)
+        turn("h0", s, [("h", s, 0)])
+        turn("y", s - 2, [("yb", s - 2, 0), ("yb", s - 2, 1)])
+        empty("h0", s)
+        product("z", "C", s - 1, 0, h_acts(s - 1))
+        joint(s, 1)
+        product("z", "C", s - 1, 1, h_acts(s - 1))
+        empty("y", s - 2)
+        quant("h0", s)
+        turn("h1", s, [("h", s, 1)])
+        add_bias(s - 1, 0)
+        empty("h1", s)
+        quant_y(s - 2)
+        product("r", "R", s, 0, q_acts(s))
+        product("r", "R", s, 1, q_acts(s))
+        add_bias(s - 1, 1)
+        product("z", "C", s, 0, h_last, [0])
+        quant("h1", s)
+        sigmoid(s, 0)
+        product("z", "C", s, 1, h_last, [0])
+        product("z", "C", s, 0, h_last, [1])
+        product("z", "C", s, 1, h_last, [1])
+        apply_mask(s - 1, 0)
+        sigmoid(s, 1)
+        apply_mask(s - 1, 1)
+        round_y(s - 1, 0)
+        add_bias(s, 0)
+        round_y(s - 1, 1)
+        add_bias(s, 1)
+        turn("y", s - 1, [("yb", s - 1, 0), ("yb", s - 1, 1)])
+        apply_mask(s, 0)
+        empty("y", s - 1)
+        mask_to_bf16(s, 1)
+        round_y(s, 0)
+        apply_mask(s, 1)
+        turn("y1", s, [("yb", s, 1)])
+        turn("y0", s, [("yb", s, 0)])
+        empty("y1", s)
+        empty("y0", s)
+        quant_y(s - 1)
+        quant_y_half(s, 1)
+        quant_y_half(s, 0)
+        store_y_scales(y_scales_last, early * P, 2 * P, [nc.scalar, nc.sync])

@@ -53,15 +53,16 @@ def tile_grouped_vqa_fusion_b12_kernel(tc, V_bytes, V_scale, Q_bytes, Q_scale, U
                    "R": (R_words, R_scales, 1), "C": (C_words, C_scales, 2)}
 
         ident = ktile([P, P], F32, "ident")
-        make_identity(nc, ident[:])
 
         def clear_plane(w, slot):
             plane = ktile([P, weights[w][2] * F], U8, "%s_plane%d" % (w, slot))
             nc.vector.memset(plane[:].bitcast(I32), 0)
             st[w, "plane", slot] = plane
 
-        for w in ("R", "U", "W", "C"):
+        for w in ("U", "R", "W", "C"):
             clear_plane(w, 0)
+        nc.vector.memset(ident[:], 0.0)
+        make_identity(nc, ident[:], nomemset=True)
 
         last = TILES - 1
         early = TILES - 2
@@ -78,11 +79,12 @@ def tile_grouped_vqa_fusion_b12_kernel(tc, V_bytes, V_scale, Q_bytes, Q_scale, U
             nc.sync.dma_start(out=t[:], in_=V_bytes[i // 2, (i % 2) * P:(i % 2 + 1) * P, :])
             st["vb", i] = t
 
-        def load_q(e):
-            t = ktile([P, 4 * KQ], U8, "q_bytes%d" % e)
-            nc.sync.dma_start(out=t[:].rearrange("p (i k) -> p i k", i=4),
-                              in_=Q_bytes.rearrange("e (h p) k -> p (e h) k", p=P)[:, 4 * e:4 * e + 4, :])
-            st["qb", e] = t
+        def load_q(first, count):
+            t = ktile([P, count * KQ], U8, "q_bytes%d" % first)
+            nc.sync.dma_start(out=t[:].rearrange("p (i k) -> p i k", i=count),
+                              in_=Q_bytes.rearrange("e (h p) k -> p (e h) k", p=P)[:, first:first + count, :])
+            for i in range(count):
+                st["qb", first + i] = (t, i * KQ)
 
         def load_act_scales(src, key, first, count):
             nb = src.shape[2]
@@ -94,7 +96,7 @@ def tile_grouped_vqa_fusion_b12_kernel(tc, V_bytes, V_scale, Q_bytes, Q_scale, U
 
         def load_words(w, e):
             words, scales, passes = weights[w]
-            t = wtile([P, passes * 2 * F], U8, w + "_words", 2 if w == "U" else 3)
+            t = wtile([P, passes * 2 * F], U8, w + "_words", 3)
             nc.sync.dma_start(out=t[:].bitcast(I32).rearrange("p (g n) -> p g n", g=passes),
                               in_=words.bitcast(I32)[passes * e:passes * (e + 1)].rearrange("g p n -> p g n"))
             for g in range(passes):
@@ -134,7 +136,7 @@ def tile_grouped_vqa_fusion_b12_kernel(tc, V_bytes, V_scale, Q_bytes, Q_scale, U
                 sc, col = st["vs", i]
                 col = col + 4 * g
             else:
-                src, base = st["qb", i // 4], (i % 4) * KQ
+                src, base = st["qb", i]
                 sc, col = st["qs", i]
             wide = wtile([P, KP], BF16, "wide%d" % g, 2)
             dst = wide[:].rearrange("t (u p e) -> t p u e", u=2, e=2)
@@ -168,8 +170,8 @@ def tile_grouped_vqa_fusion_b12_kernel(tc, V_bytes, V_scale, Q_bytes, Q_scale, U
             if not live(i):
                 return
             grouped, n = st["grouped", key, i]
-            codes = wtile([P, n * P], U32, "codes_" + key, 3)
-            scales = wtile([P, n * P], U8, "scales_" + key, 3)
+            codes = wtile([P, n * P], U32, "codes_" + key, 2)
+            scales = wtile([P, n * P], U8, "scales_" + key, 2)
             nc.vector.quantize_mx(out=codes[:].bitcast(FP8X4), scales=scales[:], in_=grouped[:])
             for j in range(n):
                 st["mx", key, i, j] = (codes[:, j * P:(j + 1) * P], scales[:, j * P:(j + 1) * P])
@@ -232,10 +234,12 @@ def tile_grouped_vqa_fusion_b12_kernel(tc, V_bytes, V_scale, Q_bytes, Q_scale, U
         def apply_mask(i, j):
             if not live(i):
                 return
-            y = wtile([P, N], F32, "y%d" % j, 3)
+            y = wtile([P, N], F32, "y%d" % j, 6)
             nc.vector.tensor_tensor(out=y[:], in0=st["biased", i, j][:], in1=st["mask", i, j][:], op=ALU.mult)
-            nc.sync.dma_start(out=out_0[i // 2, (i % 2) * P:(i % 2 + 1) * P, j * N:(j + 1) * N], in_=y[:])
             st["y", i, j] = y
+
+        def store_y(i, j):
+            nc.sync.dma_start(out=out_0[i // 2, (i % 2) * P:(i % 2 + 1) * P, j * N:(j + 1) * N], in_=st["y", i, j][:])
 
         def round_y(i, j):
             if not live(i):
@@ -268,13 +272,16 @@ def tile_grouped_vqa_fusion_b12_kernel(tc, V_bytes, V_scale, Q_bytes, Q_scale, U
             if not live(i):
                 return
             grouped, n = st["grouped", "y", i]
-            codes = wtile([P, 2 * P], U32, "y_codes", 4)
+            codes = wtile([P, 2 * P], U32, "y_codes", 6)
             for j in range(2):
                 nc.vector.quantize_mx(out=codes[:, j * P:(j + 1) * P].bitcast(FP8X4), scales=y_scales(i, j),
                                       in_=grouped[:, j * KP:(j + 1) * KP])
+            st["y_codes", i] = codes
+
+        def store_codes(i):
             dst = out_1.rearrange("g p m t -> p g (m t)").bitcast(I32)
             nc.sync.dma_start(out=dst[:, :, i * P:(i + 1) * P],
-                              in_=codes[:].bitcast(I32).rearrange("p (g m) -> p g m", g=2))
+                              in_=st["y_codes", i][:].bitcast(I32).rearrange("p (g m) -> p g m", g=2))
             if i == early - 1:
                 store_y_scales(y_scales_early, 0, early * P, [nc.sync])
 
@@ -296,24 +303,6 @@ def tile_grouped_vqa_fusion_b12_kernel(tc, V_bytes, V_scale, Q_bytes, Q_scale, U
                            in_=st["c_bank", e][:].rearrange("t (j p) -> t p j", j=4))
             st["c_rows", e] = rows
 
-        load_q(0)
-        load_act_scales(Q_scale, "qs", 0, 4)
-        load_v(0)
-        load_act_scales(V_scale, "vs", 0, 4)
-        load_v(1)
-        load_words("R", 0)
-        load_words_half("U", 0, 0)
-        load_planes("R", 0)
-        load_planes("U", 0)
-        load_words("W", 0)
-        load_v(2)
-        load_planes("W", 0)
-        load_words_half("U", 0, 1)
-        load_c()
-        load_v(3)
-        load_words("C", 0)
-        load_planes("C", 0)
-
         def q_acts(i):
             return [("mx", "q", i, 0)]
 
@@ -323,143 +312,166 @@ def tile_grouped_vqa_fusion_b12_kernel(tc, V_bytes, V_scale, Q_bytes, Q_scale, U
         def turn_v(i, half):
             turn("v%d" % half, i, [("wide", i, 2 * half), ("wide", i, 2 * half + 1)])
 
-        widen(0, 4)
-        turn("q", 0, [("wide", 0, 4)])
-        empty("q", 0)
+        def turn_h(i):
+            turn("h", i, [("h", i, 0), ("h", i, 1)])
+
+        def turn_y(i):
+            turn("y", i, [("yb", i, 0), ("yb", i, 1)])
+
+        def bundle(load, e):
+            load("C", e - 1)
+            for w in ("U", "W", "R"):
+                load(w, e)
+
+        load_v(0)
+        load_act_scales(V_scale, "vs", 0, 2)
+        load_q(0, 2)
+        load_act_scales(Q_scale, "qs", 0, 2)
+        load_words_half("U", 0, 0)
+        load_planes("U", 0)
+        load_v(1)
+        load_words("R", 0)
+        load_planes("R", 0)
+        load_words_half("U", 0, 1)
+        load_words("W", 0)
+        load_planes("W", 0)
+        load_v(2)
+        load_act_scales(V_scale, "vs", 2, TILES - 2)
+        load_q(2, 2)
+        load_act_scales(Q_scale, "qs", 2, TILES - 2)
+        load_c()
+        load_v(3)
+        bundle(load_words, 1)
+
         for half in range(2):
             widen(0, 2 * half)
             widen(0, 2 * half + 1)
             turn_v(0, half)
             empty("v%d" % half, 0)
-        quant("q", 0)
+        widen(0, 4)
+        turn("q", 0, [("wide", 0, 4)])
         quant("v0", 0)
+        empty("q", 0)
+        product("a", "U", 0, 0, v_acts(0), [0, 1])
+        quant("v1", 0)
+        product("a", "U", 0, 0, v_acts(0), [2, 3])
+        quant("q", 0)
+        for g in range(5):
+            widen(1, g)
         product("r", "R", 0, 0, q_acts(0))
         product("r", "R", 0, 1, q_acts(0))
-        widen(1, 4)
-        quant("v1", 0)
         sigmoid(0, 0)
         sigmoid(0, 1)
-        for g in range(4):
-            widen(1, g)
-        for w in ("U", "W", "R", "C"):
-            clear_plane(w, 1)
-        for w in ("U", "W", "R"):
-            load_words(w, 1)
-        for w in ("U", "W", "R"):
-            load_planes(w, 1)
-        load_v(4)
-        load_act_scales(V_scale, "vs", 4, 4)
-        load_q(1)
-        load_act_scales(Q_scale, "qs", 4, 4)
-        load_words("C", 1)
-        load_planes("C", 1)
-        load_v(5)
-        for w in ("U", "W", "R", "C"):
-            load_words(w, 2)
-        load_v(6)
-        load_v(7)
-        product("a", "U", 0, 0, v_acts(0))
-        product("b", "W", 0, 0, q_acts(0))
         tanh(0, 0)
         turn_v(1, 0)
         turn_v(1, 1)
         turn("q", 1, [("wide", 1, 4)])
-        empty("v0", 1)
-        widen(2, 0)
-        joint(0, 0)
+        for w in ("U", "W", "R", "C"):
+            clear_plane(w, 1)
+        bundle(load_planes, 1)
+        load_v(4)
+        load_q(4, 4)
+        load_v(5)
+        bundle(load_words, 2)
         product("a", "U", 0, 1, v_acts(0))
+        empty("v0", 1)
         empty("v1", 1)
-        empty("q", 1)
+        product("b", "W", 0, 0, q_acts(0))
         product("b", "W", 0, 1, q_acts(0))
-        widen(2, 1)
+        empty("q", 1)
         quant("v0", 1)
         tanh(0, 1)
         quant("v1", 1)
-        widen(2, 2)
-        joint(0, 1)
+        joint(0, 0)
         quant("q", 1)
-        widen(2, 3)
-        widen(2, 4)
+        widen(2, 0)
+        joint(0, 1)
+        widen(2, 1)
 
         for s in range(1, last):
-            if s in (2, 4):
-                for w in ("U", "W", "R"):
-                    load_planes(w, s // 2 + 1)
-            if s in (3, 5):
-                load_planes("C", s // 2 + 1)
             if s == 2:
-                for w in ("W", "R"):
-                    load_words(w, 3)
-            if s == 3:
-                load_words("C", 3)
+                bundle(load_planes, 2)
+                load_v(6)
+                load_v(7)
+                bundle(load_words, 3)
             if s == 4:
-                load_words("U", 3)
+                bundle(load_planes, 3)
+                load_words("C", 3)
+            if s == 5:
+                load_planes("C", 3)
             n, o = s + 1, s - 2
-            turn("h", s - 1, [("h", s - 1, 0), ("h", s - 1, 1)])
-            add_bias(o, 1)
-            turn_v(n, 0)
-            empty("h", s - 1)
-            turn_v(n, 1)
-            apply_mask(o, 0)
-            turn("q", n, [("wide", n, 4)])
-            turn("y", s - 3, [("yb", s - 3, 0), ("yb", s - 3, 1)])
-            empty("v0", n)
-            spread_turn(s - 1)
-            quant("h", s - 1)
-            widen(s + 2, 0)
-            empty("v1", n)
-            apply_mask(o, 1)
             product("a", "U", s, 0, v_acts(s))
-            empty("q", n)
-            quant("v0", n)
-            quant("v1", n)
-            empty("y", s - 3)
-            spread_empty(s - 1)
+            add_bias(o, 1)
+            apply_mask(o, 0)
             product("b", "W", s, 0, q_acts(s))
             tanh(s, 0)
-            widen(s + 2, 1)
-            quant_y(s - 3)
+            widen(n, 2)
+            apply_mask(o, 1)
             product("a", "U", s, 1, v_acts(s))
             round_y(o, 0)
-            joint(s, 0)
-            product("b", "W", s, 1, q_acts(s))
-            quant("q", n)
-            widen(s + 2, 2)
-            tanh(s, 1)
-            product("r", "R", s, 0, q_acts(s))
-            widen(s + 2, 3)
-            product("r", "R", s, 1, q_acts(s))
+            widen(n, 3)
+            widen(n, 4)
             round_y(o, 1)
+            joint(s, 0)
+            turn_h(s - 1)
+            tanh(s, 1)
+            turn_v(n, 0)
+            quant_y(s - 3)
+            empty("h", s - 1)
+            turn_v(n, 1)
+            turn("q", n, [("wide", n, 4)])
+            turn_y(o)
+            empty("v0", n)
+            spread_turn(s - 1)
+            widen(n + 1, 0)
+            widen(n + 1, 1)
+            product("b", "W", s, 1, q_acts(s))
+            quant("h", s - 1)
+            empty("v1", n)
+            product("r", "R", s, 0, q_acts(s))
             joint(s, 1)
+            empty("q", n)
+            product("r", "R", s, 1, q_acts(s))
+            empty("y", o)
+            spread_empty(s - 1)
             product("z", "C", s - 1, 0, h_acts(s - 1))
+            quant("v0", n)
+            quant("v1", n)
             sigmoid(s, 0)
-            widen(s + 2, 4)
             product("z", "C", s - 1, 1, h_acts(s - 1))
+            quant("q", n)
             sigmoid(s, 1)
             add_bias(s - 1, 0)
+            if s >= 4:
+                for i in (range(o + 1) if s == 4 else [o]):
+                    store_y(i, 0)
+                    store_y(i, 1)
+                for i in (range(o) if s == 4 else [o - 1]):
+                    store_codes(i)
 
         s = last
         h_last = [("mx", "h0", s, 0), ("mx", "h1", s, 0)]
-        turn("h", s - 1, [("h", s - 1, 0), ("h", s - 1, 1)])
+        turn_h(s - 1)
         add_bias(s - 2, 1)
         empty("h", s - 1)
         apply_mask(s - 2, 0)
-        turn("y", s - 3, [("yb", s - 3, 0), ("yb", s - 3, 1)])
+        store_y(s - 2, 0)
+        product("a", "U", s, 0, v_acts(s))
         quant("h", s - 1)
         apply_mask(s - 2, 1)
-        product("a", "U", s, 0, v_acts(s))
-        empty("y", s - 3)
+        store_y(s - 2, 1)
         round_y(s - 2, 0)
         product("b", "W", s, 0, q_acts(s))
         tanh(s, 0)
         quant_y(s - 3)
+        store_codes(s - 3)
         product("a", "U", s, 1, v_acts(s))
         round_y(s - 2, 1)
         joint(s, 0)
         product("b", "W", s, 1, q_acts(s))
         tanh(s, 1)
         turn("h0", s, [("h", s, 0)])
-        turn("y", s - 2, [("yb", s - 2, 0), ("yb", s - 2, 1)])
+        turn_y(s - 2)
         empty("h0", s)
         product("z", "C", s - 1, 0, h_acts(s - 1))
         joint(s, 1)
@@ -470,6 +482,7 @@ def tile_grouped_vqa_fusion_b12_kernel(tc, V_bytes, V_scale, Q_bytes, Q_scale, U
         add_bias(s - 1, 0)
         empty("h1", s)
         quant_y(s - 2)
+        store_codes(s - 2)
         product("r", "R", s, 0, q_acts(s))
         product("r", "R", s, 1, q_acts(s))
         add_bias(s - 1, 1)
@@ -480,23 +493,28 @@ def tile_grouped_vqa_fusion_b12_kernel(tc, V_bytes, V_scale, Q_bytes, Q_scale, U
         product("z", "C", s, 0, h_last, [1])
         product("z", "C", s, 1, h_last, [1])
         apply_mask(s - 1, 0)
+        store_y(s - 1, 0)
         sigmoid(s, 1)
         apply_mask(s - 1, 1)
+        store_y(s - 1, 1)
         round_y(s - 1, 0)
         add_bias(s, 0)
         round_y(s - 1, 1)
         add_bias(s, 1)
-        turn("y", s - 1, [("yb", s - 1, 0), ("yb", s - 1, 1)])
+        turn_y(s - 1)
         apply_mask(s, 0)
+        store_y(s, 0)
         empty("y", s - 1)
         mask_to_bf16(s, 1)
         round_y(s, 0)
         apply_mask(s, 1)
+        store_y(s, 1)
         turn("y1", s, [("yb", s, 1)])
         turn("y0", s, [("yb", s, 0)])
         empty("y1", s)
         empty("y0", s)
         quant_y(s - 1)
+        store_codes(s - 1)
         quant_y_half(s, 1)
         quant_y_half(s, 0)
         store_y_scales(y_scales_last, early * P, 2 * P, [nc.scalar, nc.sync])

@@ -128,6 +128,10 @@ def tile_grouped_vqa_fusion_b12_kernel(tc, V_bytes, V_scale, Q_bytes, Q_scale, U
         def live(i):
             return 0 <= i < TILES
 
+        def word_blocks(t):
+            words = t[:].bitcast(F32)
+            return [words[:, u * P:(u + 1) * P] for u in range(2)]
+
         def widen(i, g):
             if not live(i):
                 return
@@ -138,23 +142,22 @@ def tile_grouped_vqa_fusion_b12_kernel(tc, V_bytes, V_scale, Q_bytes, Q_scale, U
             else:
                 src, base = st["qb", i]
                 sc, col = st["qs", i]
-            wide = wtile([P, KP], BF16, "wide%d" % g, 2)
+            wide = wtile([P, KP], BF16, "wide%d" % g, 3)
             dst = wide[:].rearrange("t (u p e) -> t p u e", u=2, e=2)
             for q in range(4):
                 blk = src[:, base + q * BLK:base + (q + 1) * BLK].bitcast(FP8)
                 nc.vector.tensor_scalar(out=dst[:, 32 * q:32 * (q + 1)],
                                         in0=blk.rearrange("t (p u e) -> t p u e", u=2, e=2),
                                         scalar1=sc[:, col + q:col + q + 1], scalar2=None, op0=ALU.mult)
-            st["wide", i, g] = wide
+            st["wide", i, g] = word_blocks(wide)
 
         def turn(key, i, srcs):
             if not live(i):
                 return
             b = bank()
             for j, k in enumerate(srcs):
-                words = st[k][:].bitcast(F32)
                 for u in range(2):
-                    nc.tensor.transpose(b[:, (2 * j + u) * P:(2 * j + u + 1) * P], words[:, u * P:(u + 1) * P], ident[:])
+                    nc.tensor.transpose(b[:, (2 * j + u) * P:(2 * j + u + 1) * P], st[k][u], ident[:])
             st["turned", key, i] = (b, len(srcs))
 
         def empty(key, i):
@@ -201,12 +204,18 @@ def tile_grouped_vqa_fusion_b12_kernel(tc, V_bytes, V_scale, Q_bytes, Q_scale, U
         def plain(ap):
             return ap.rearrange("t (u p e) -> t u p e", u=2, e=2)
 
+        def row_tile(key, i, dtype, bufs):
+            if (key, i) not in st:
+                st[key, i] = wtile([P, A], dtype, key, bufs)
+            return st[key, i]
+
+        def cols(j):
+            return slice(0, A) if j is None else slice(j * N, (j + 1) * N)
+
         def sigmoid(i, j):
             if not live(i):
                 return
-            s = wtile([P, N], F32, "mask%d" % j, 3)
-            nc.scalar.activation(out=s[:], in_=st["r", i, j][:], func=ACT.Sigmoid)
-            st["mask", i, j] = s
+            nc.scalar.activation(out=row_tile("mask", i, F32, 3)[:, cols(j)], in_=st["r", i, j][:], func=ACT.Sigmoid)
 
         def tanh(i, j):
             if not live(i):
@@ -221,32 +230,38 @@ def tile_grouped_vqa_fusion_b12_kernel(tc, V_bytes, V_scale, Q_bytes, Q_scale, U
             h = wtile([P, N], BF16, "joint%d" % j, 2)
             nc.vector.tensor_tensor(out=plain(h[:]), in0=paired(st["b", i, j][:]), in1=plain(st["tanh", i, j][:]),
                                     op=ALU.mult)
-            st["h", i, j] = h
+            st["h", i, j] = word_blocks(h)
 
         def add_bias(i, j):
             if not live(i):
                 return
-            t = wtile([P, N], F32, "biased%d" % j, 2)
-            nc.vector.tensor_tensor(out=t[:], in0=st["z", i, j][:], in1=st["c_rows", i // 2][:, j * N:(j + 1) * N],
-                                    op=ALU.add)
-            st["biased", i, j] = t
+            nc.vector.tensor_tensor(out=row_tile("biased", i, F32, 2)[:, cols(j)], in0=st["z", i, j][:],
+                                    in1=st["c_rows", i // 2][:, cols(j)], op=ALU.add)
 
-        def apply_mask(i, j):
+        def apply_mask(i, j=None):
             if not live(i):
                 return
-            y = wtile([P, N], F32, "y%d" % j, 6)
-            nc.vector.tensor_tensor(out=y[:], in0=st["biased", i, j][:], in1=st["mask", i, j][:], op=ALU.mult)
-            st["y", i, j] = y
+            nc.vector.tensor_tensor(out=row_tile("y", i, F32, 6)[:, cols(j)], in0=st["biased", i][:, cols(j)],
+                                    in1=st["mask", i][:, cols(j)], op=ALU.mult)
 
-        def store_y(i, j):
-            nc.sync.dma_start(out=out_0[i // 2, (i % 2) * P:(i % 2 + 1) * P, j * N:(j + 1) * N], in_=st["y", i, j][:])
+        def store_y(i, j=None):
+            nc.sync.dma_start(out=out_0[i // 2, (i % 2) * P:(i % 2 + 1) * P, cols(j)], in_=st["y", i][:, cols(j)])
 
-        def round_y(i, j):
+        def round_y(i):
             if not live(i):
                 return
-            yb = wtile([P, N], BF16, "y_bf%d" % j, 2)
-            nc.scalar.copy(out=plain(yb[:]), in_=paired(st["y", i, j][:]))
-            st["yb", i, j] = yb
+            yb = wtile([P, A], BF16, "y_bf", 2)
+            nc.scalar.copy(out=plain(yb[:]), in_=paired(st["y", i][:]))
+            words = yb[:].bitcast(F32)
+            for j in range(2):
+                st["yb", i, j] = [words[:, (2 * u + j) * P:(2 * u + j + 1) * P] for u in range(2)]
+
+        def round_y_half(i, j):
+            if not live(i):
+                return
+            yb = wtile([P, N], BF16, "y_bf_half", 4)
+            nc.scalar.copy(out=plain(yb[:]), in_=paired(st["y", i][:, cols(j)]))
+            st["yb", i, j] = word_blocks(yb)
 
         def store_y_scales(plane, m0, width, queues):
             rows = out_2.bitcast(I32).rearrange("g (q r) m -> r q g m", r=4)
@@ -255,10 +270,10 @@ def tile_grouped_vqa_fusion_b12_kernel(tc, V_bytes, V_scale, Q_bytes, Q_scale, U
                                   in_=plane[r:P:32, :].bitcast(I32).rearrange("q (g m) -> q g m", g=2))
 
         def mask_to_bf16(i, j):
-            yb = wtile([P, N], BF16, "y_bf%d" % j, 2)
-            nc.vector.tensor_tensor(out=plain(yb[:]), in0=paired(st["biased", i, j][:]),
-                                    in1=paired(st["mask", i, j][:]), op=ALU.mult)
-            st["yb", i, j] = yb
+            yb = wtile([P, N], BF16, "y_bf_half", 4)
+            nc.vector.tensor_tensor(out=plain(yb[:]), in0=paired(st["biased", i][:, cols(j)]),
+                                    in1=paired(st["mask", i][:, cols(j)]), op=ALU.mult)
+            st["yb", i, j] = word_blocks(yb)
 
         def quant_y_half(i, j):
             grouped, n = st["grouped", "y%d" % j, i]
@@ -318,10 +333,9 @@ def tile_grouped_vqa_fusion_b12_kernel(tc, V_bytes, V_scale, Q_bytes, Q_scale, U
         def turn_y(i):
             turn("y", i, [("yb", i, 0), ("yb", i, 1)])
 
-        def bundle(load, e):
-            load("C", e - 1)
-            for w in ("U", "W", "R"):
-                load(w, e)
+        def load_pair(load, e, first):
+            for w, group in ([("C", e - 1), ("U", e)] if first else [("W", e), ("R", e)]):
+                load(w, group)
 
         load_v(0)
         load_act_scales(V_scale, "vs", 0, 2)
@@ -341,7 +355,7 @@ def tile_grouped_vqa_fusion_b12_kernel(tc, V_bytes, V_scale, Q_bytes, Q_scale, U
         load_act_scales(Q_scale, "qs", 2, TILES - 2)
         load_c()
         load_v(3)
-        bundle(load_words, 1)
+        load_pair(load_words, 1, True)
 
         for half in range(2):
             widen(0, 2 * half)
@@ -350,6 +364,8 @@ def tile_grouped_vqa_fusion_b12_kernel(tc, V_bytes, V_scale, Q_bytes, Q_scale, U
             empty("v%d" % half, 0)
         widen(0, 4)
         turn("q", 0, [("wide", 0, 4)])
+        for w in ("R", "W", "C"):
+            clear_plane(w, 1)
         quant("v0", 0)
         empty("q", 0)
         product("a", "U", 0, 0, v_acts(0), [0, 1])
@@ -358,44 +374,52 @@ def tile_grouped_vqa_fusion_b12_kernel(tc, V_bytes, V_scale, Q_bytes, Q_scale, U
         quant("q", 0)
         for g in range(5):
             widen(1, g)
+        clear_plane("U", 1)
         product("r", "R", 0, 0, q_acts(0))
         product("r", "R", 0, 1, q_acts(0))
         sigmoid(0, 0)
         sigmoid(0, 1)
-        tanh(0, 0)
         turn_v(1, 0)
         turn_v(1, 1)
         turn("q", 1, [("wide", 1, 4)])
-        for w in ("U", "W", "R", "C"):
-            clear_plane(w, 1)
-        bundle(load_planes, 1)
+        load_pair(load_planes, 1, True)
         load_v(4)
+        load_pair(load_words, 1, False)
+        load_pair(load_planes, 1, False)
         load_q(4, 4)
         load_v(5)
-        bundle(load_words, 2)
-        product("a", "U", 0, 1, v_acts(0))
+        load_pair(load_words, 2, True)
+        load_pair(load_words, 2, False)
+        load_v(6)
         empty("v0", 1)
+        tanh(0, 0)
+        product("a", "U", 0, 1, v_acts(0))
         empty("v1", 1)
         product("b", "W", 0, 0, q_acts(0))
         product("b", "W", 0, 1, q_acts(0))
         empty("q", 1)
+        widen(2, 0)
+        widen(2, 1)
+        widen(2, 2)
         quant("v0", 1)
         tanh(0, 1)
         quant("v1", 1)
         joint(0, 0)
         quant("q", 1)
-        widen(2, 0)
+        widen(2, 3)
         joint(0, 1)
-        widen(2, 1)
 
+        spread = {1: [0, 1], 2: [2], 3: [3]}
         for s in range(1, last):
             if s == 2:
-                bundle(load_planes, 2)
-                load_v(6)
+                load_pair(load_planes, 2, True)
+                load_pair(load_planes, 2, False)
                 load_v(7)
-                bundle(load_words, 3)
+                load_pair(load_words, 3, True)
+                load_pair(load_words, 3, False)
             if s == 4:
-                bundle(load_planes, 3)
+                load_pair(load_planes, 3, True)
+                load_pair(load_planes, 3, False)
                 load_words("C", 3)
             if s == 5:
                 load_planes("C", 3)
@@ -405,26 +429,27 @@ def tile_grouped_vqa_fusion_b12_kernel(tc, V_bytes, V_scale, Q_bytes, Q_scale, U
             apply_mask(o, 0)
             product("b", "W", s, 0, q_acts(s))
             tanh(s, 0)
-            widen(n, 2)
+            widen(n + 1, 0)
             apply_mask(o, 1)
             product("a", "U", s, 1, v_acts(s))
-            round_y(o, 0)
-            widen(n, 3)
+            round_y_half(o, 0)
+            round_y_half(o, 1)
+            widen(n + 1, 1)
             widen(n, 4)
-            round_y(o, 1)
             joint(s, 0)
             turn_h(s - 1)
-            tanh(s, 1)
+            empty("h", s - 1)
             turn_v(n, 0)
             quant_y(s - 3)
-            empty("h", s - 1)
+            tanh(s, 1)
             turn_v(n, 1)
             turn("q", n, [("wide", n, 4)])
             turn_y(o)
             empty("v0", n)
-            spread_turn(s - 1)
-            widen(n + 1, 0)
-            widen(n + 1, 1)
+            for e in spread.get(s, []):
+                spread_turn(e)
+            widen(n + 1, 2)
+            widen(n + 1, 3)
             product("b", "W", s, 1, q_acts(s))
             quant("h", s - 1)
             empty("v1", n)
@@ -433,7 +458,8 @@ def tile_grouped_vqa_fusion_b12_kernel(tc, V_bytes, V_scale, Q_bytes, Q_scale, U
             empty("q", n)
             product("r", "R", s, 1, q_acts(s))
             empty("y", o)
-            spread_empty(s - 1)
+            for e in spread.get(s, []):
+                spread_empty(e)
             product("z", "C", s - 1, 0, h_acts(s - 1))
             quant("v0", n)
             quant("v1", n)
@@ -444,8 +470,7 @@ def tile_grouped_vqa_fusion_b12_kernel(tc, V_bytes, V_scale, Q_bytes, Q_scale, U
             add_bias(s - 1, 0)
             if s >= 4:
                 for i in (range(o + 1) if s == 4 else [o]):
-                    store_y(i, 0)
-                    store_y(i, 1)
+                    store_y(i)
                 for i in (range(o) if s == 4 else [o - 1]):
                     store_codes(i)
 
@@ -454,59 +479,57 @@ def tile_grouped_vqa_fusion_b12_kernel(tc, V_bytes, V_scale, Q_bytes, Q_scale, U
         turn_h(s - 1)
         add_bias(s - 2, 1)
         empty("h", s - 1)
-        apply_mask(s - 2, 0)
-        store_y(s - 2, 0)
         product("a", "U", s, 0, v_acts(s))
-        quant("h", s - 1)
-        apply_mask(s - 2, 1)
-        store_y(s - 2, 1)
-        round_y(s - 2, 0)
-        product("b", "W", s, 0, q_acts(s))
-        tanh(s, 0)
+        apply_mask(s - 2, 0)
         quant_y(s - 3)
         store_codes(s - 3)
+        product("b", "W", s, 0, q_acts(s))
+        tanh(s, 0)
+        quant("h", s - 1)
+        apply_mask(s - 2, 1)
+        store_y(s - 2)
         product("a", "U", s, 1, v_acts(s))
-        round_y(s - 2, 1)
+        round_y_half(s - 2, 0)
+        product("z", "C", s - 1, 0, h_acts(s - 1))
         joint(s, 0)
-        product("b", "W", s, 1, q_acts(s))
         tanh(s, 1)
+        product("b", "W", s, 1, q_acts(s))
+        product("z", "C", s - 1, 1, h_acts(s - 1))
+        add_bias(s - 1, 0)
+        round_y_half(s - 2, 1)
         turn("h0", s, [("h", s, 0)])
         turn_y(s - 2)
-        empty("h0", s)
-        product("z", "C", s - 1, 0, h_acts(s - 1))
         joint(s, 1)
-        product("z", "C", s - 1, 1, h_acts(s - 1))
+        empty("h0", s)
         empty("y", s - 2)
-        quant("h0", s)
-        turn("h1", s, [("h", s, 1)])
-        add_bias(s - 1, 0)
-        empty("h1", s)
-        quant_y(s - 2)
-        store_codes(s - 2)
         product("r", "R", s, 0, q_acts(s))
         product("r", "R", s, 1, q_acts(s))
         add_bias(s - 1, 1)
+        turn("h1", s, [("h", s, 1)])
+        quant("h0", s)
+        empty("h1", s)
+        apply_mask(s - 1, 0)
         product("z", "C", s, 0, h_last, [0])
+        product("z", "C", s, 1, h_last, [0])
         quant("h1", s)
         sigmoid(s, 0)
-        product("z", "C", s, 1, h_last, [0])
         product("z", "C", s, 0, h_last, [1])
         product("z", "C", s, 1, h_last, [1])
-        apply_mask(s - 1, 0)
-        store_y(s - 1, 0)
-        sigmoid(s, 1)
         apply_mask(s - 1, 1)
-        store_y(s - 1, 1)
-        round_y(s - 1, 0)
+        sigmoid(s, 1)
+        store_y(s - 1)
+        quant_y(s - 2)
+        store_codes(s - 2)
+        round_y_half(s - 1, 0)
         add_bias(s, 0)
-        round_y(s - 1, 1)
+        round_y_half(s - 1, 1)
         add_bias(s, 1)
         turn_y(s - 1)
         apply_mask(s, 0)
         store_y(s, 0)
         empty("y", s - 1)
         mask_to_bf16(s, 1)
-        round_y(s, 0)
+        round_y_half(s, 0)
         apply_mask(s, 1)
         store_y(s, 1)
         turn("y1", s, [("yb", s, 1)])

@@ -151,6 +151,24 @@ def tile_grouped_vqa_fusion_b12_kernel(tc, V_bytes, V_scale, Q_bytes, Q_scale, U
                                         scalar1=sc[:, col + q:col + q + 1], scalar2=None, op0=ALU.mult)
             st["wide", i, g] = word_blocks(wide)
 
+        def widen_q(i, blocks):
+            if not live(i):
+                return
+            src, base = st["qb", i]
+            sc, col = st["qs", i]
+            if ("wide_q", i) not in st:
+                st["wide_q", i] = wtile([P, KP], BF16, "wide4", 3)
+            wide = st["wide_q", i]
+            st["wide", i, 4] = [wide[:].bitcast(F32)[:, u:2 * P:2] for u in range(2)]
+            for q in blocks:
+                blk = src[:, base + q * BLK:base + (q + 1) * BLK].bitcast(FP8)
+                if q < 2 and i > 1:
+                    nc.scalar.activation(out=wide[:, q * BLK:(q + 1) * BLK], in_=blk,
+                                         func=ACT.Copy, scale=sc[:, col + q:col + q + 1])
+                else:
+                    nc.vector.tensor_scalar(out=wide[:, q * BLK:(q + 1) * BLK], in0=blk,
+                                            scalar1=sc[:, col + q:col + q + 1], scalar2=None, op0=ALU.mult)
+
         def turn(key, i, srcs):
             if not live(i):
                 return
@@ -362,7 +380,7 @@ def tile_grouped_vqa_fusion_b12_kernel(tc, V_bytes, V_scale, Q_bytes, Q_scale, U
             widen(0, 2 * half + 1)
             turn_v(0, half)
             empty("v%d" % half, 0)
-        widen(0, 4)
+        widen_q(0, range(4))
         turn("q", 0, [("wide", 0, 4)])
         for w in ("R", "W", "C"):
             clear_plane(w, 1)
@@ -372,8 +390,9 @@ def tile_grouped_vqa_fusion_b12_kernel(tc, V_bytes, V_scale, Q_bytes, Q_scale, U
         quant("v1", 0)
         product("a", "U", 0, 0, v_acts(0), [2, 3])
         quant("q", 0)
-        for g in range(5):
+        for g in range(4):
             widen(1, g)
+        widen_q(1, range(4))
         clear_plane("U", 1)
         product("r", "R", 0, 0, q_acts(0))
         product("r", "R", 0, 1, q_acts(0))
@@ -428,6 +447,7 @@ def tile_grouped_vqa_fusion_b12_kernel(tc, V_bytes, V_scale, Q_bytes, Q_scale, U
             add_bias(o, 1)
             apply_mask(o, 0)
             product("b", "W", s, 0, q_acts(s))
+            widen_q(n, range(2))
             tanh(s, 0)
             widen(n + 1, 0)
             apply_mask(o, 1)
@@ -435,7 +455,7 @@ def tile_grouped_vqa_fusion_b12_kernel(tc, V_bytes, V_scale, Q_bytes, Q_scale, U
             round_y_half(o, 0)
             round_y_half(o, 1)
             widen(n + 1, 1)
-            widen(n, 4)
+            widen_q(n, range(2, 4))
             joint(s, 0)
             turn_h(s - 1)
             empty("h", s - 1)
@@ -540,4 +560,4 @@ def tile_grouped_vqa_fusion_b12_kernel(tc, V_bytes, V_scale, Q_bytes, Q_scale, U
         store_codes(s - 1)
         quant_y_half(s, 1)
         quant_y_half(s, 0)
-        store_y_scales(y_scales_last, early * P, 2 * P, [nc.scalar, nc.sync])
+        store_y_scales(y_scales_last, early * P, 2 * P, [nc.sync])

from contextlib import ExitStack

import concourse.mybir as mybir
from concourse.masks import make_identity

G, T, KV, KQ, F, A = 4, 256, 2048, 512, 1024, 1024
FLOPS = 2 * G * T * (KV * F + KQ * F + KQ * A + F * A)

F32 = mybir.dt.float32
BF16 = mybir.dt.bfloat16
I32 = mybir.dt.int32
U32 = mybir.dt.uint32
U8 = mybir.dt.uint8
FP8 = mybir.dt.float8_e4m3fn
FP8X4 = mybir.dt.float8_e4m3fn_x4
FP4X4 = mybir.dt.float4_e2m1fn_x4
ACT = mybir.ActivationFunctionType
ALU = mybir.AluOpType

P = 128
KP = 512
N = 512
BLK = 128
TILES = G * T // P
BANKS = 8


def tile_grouped_vqa_fusion_b12_kernel(tc, V_bytes, V_scale, Q_bytes, Q_scale, U_words, U_scales,
                                                   W_words, W_scales, R_words, R_scales, C_words, C_scales, c,
                                                   out_0, out_1, out_2):
    nc = tc.nc
    with ExitStack() as ctx:
        keep = ctx.enter_context(tc.tile_pool(name="keep", bufs=1))
        work = ctx.enter_context(tc.tile_pool(name="work", bufs=2))
        psum = ctx.enter_context(tc.psum_pool(name="psum", bufs=1))
        ctx.enter_context(tc.manual_schedule())

        st = {}
        taken = []

        def bank():
            n = len(taken) % BANKS
            taken.append(n)
            return psum.tile([P, N], F32, name="bank%d" % n, tag="bank%d" % n)

        def wtile(shape, dtype, tag, bufs):
            return work.tile(shape, dtype, name=tag, tag=tag, bufs=bufs, align_bytes=64)

        def ktile(shape, dtype, tag):
            return keep.tile(shape, dtype, name=tag, tag=tag, align_bytes=64)

        weights = {"U": (U_words, U_scales, 4), "W": (W_words, W_scales, 1),
                   "R": (R_words, R_scales, 1), "C": (C_words, C_scales, 2)}

        ident = ktile([P, P], F32, "ident")

        def clear_plane(w, slot):
            plane = ktile([P, weights[w][2] * F], U8, "%s_plane%d" % (w, slot))
            nc.vector.memset(plane[:].bitcast(I32), 0)
            st[w, "plane", slot] = plane

        for w in ("U", "R", "W", "C"):
            clear_plane(w, 0)
        nc.vector.memset(ident[:], 0.0)
        make_identity(nc, ident[:], nomemset=True)

        last = TILES - 1
        early = TILES - 2
        y_scales_early = ktile([P, 2 * early * P], U8, "y_scales_early")
        y_scales_last = ktile([P, 2 * 2 * P], U8, "y_scales_last")

        def y_scales(i, j):
            if i < early:
                return y_scales_early[:, (j * early + i) * P:(j * early + i + 1) * P]
            return y_scales_last[:, (2 * j + i - early) * P:(2 * j + i - early + 1) * P]

        def load_v(i):
            t = ktile([P, KV], U8, "v_bytes%d" % i)
            nc.sync.dma_start(out=t[:], in_=V_bytes[i // 2, (i % 2) * P:(i % 2 + 1) * P, :])
            st["vb", i] = t

        def load_q(first, count):
            t = ktile([P, count * KQ], U8, "q_bytes%d" % first)
            nc.sync.dma_start(out=t[:].rearrange("p (i k) -> p i k", i=count),
                              in_=Q_bytes.rearrange("e (h p) k -> p (e h) k", p=P)[:, first:first + count, :])
            for i in range(count):
                st["qb", first + i] = (t, i * KQ)

        def load_act_scales(src, key, first, count):
            nb = src.shape[2]
            t = ktile([P, count * nb], F32, "%s%d" % (key, first))
            nc.sync.dma_start(out=t[:].rearrange("p (i j) -> p i j", j=nb),
                              in_=src.rearrange("e (h p) j -> p (e h) j", p=P)[:, first:first + count, :])
            for i in range(count):
                st[key, first + i] = (t, i * nb)

        def load_words(w, e):
            words, scales, passes = weights[w]
            t = wtile([P, passes * 2 * F], U8, w + "_words", 3)
            nc.sync.dma_start(out=t[:].bitcast(I32).rearrange("p (g n) -> p g n", g=passes),
                              in_=words.bitcast(I32)[passes * e:passes * (e + 1)].rearrange("g p n -> p g n"))
            for g in range(passes):
                for j in range(2):
                    st[w, "words", e, g, j] = t[:, 2 * (g * F + j * N):2 * (g * F + (j + 1) * N)]

        def load_words_half(w, e, j):
            words, scales, passes = weights[w]
            t = ktile([P, passes * 2 * N], U8, "%s_words_half%d" % (w, j))
            src = words.bitcast(I32)[passes * e:passes * (e + 1), :, j * N // 2:(j + 1) * N // 2]
            nc.sync.dma_start(out=t[:].bitcast(I32).rearrange("p (g n) -> p g n", g=passes),
                              in_=src.rearrange("g p n -> p g n"))
            for g in range(passes):
                st[w, "words", e, g, j] = t[:, 2 * g * N:2 * (g + 1) * N]

        def load_planes(w, e):
            words, scales, passes = weights[w]
            plane = st[w, "plane", e % 2]
            rows = scales.bitcast(I32).rearrange("g (q r) n -> r q g n", r=4)
            for r in range(4):
                nc.sync.dma_start(out=plane[r:P:32, :].bitcast(I32).rearrange("q (g n) -> q g n", g=passes),
                                  in_=rows[r, :, passes * e:passes * (e + 1), :])

        def load_c():
            t = ktile([P, G * 8], BF16, "c_cols")
            nc.sync.dma_start(out=t[:].rearrange("p (e j) -> p e j", e=G), in_=c.rearrange("e (p j) -> p e j", p=P))
            st["c_cols"] = t

        def live(i):
            return 0 <= i < TILES

        def word_blocks(t):
            words = t[:].bitcast(F32)
            return [words[:, u * P:(u + 1) * P] for u in range(2)]

        def widen(i, g):
            if not live(i):
                return
            if g < 4:
                src, base = st["vb", i], g * KP
                sc, col = st["vs", i]
                col = col + 4 * g
            else:
                src, base = st["qb", i]
                sc, col = st["qs", i]
            wide = wtile([P, KP], BF16, "wide%d" % g, 3)
            dst = wide[:].rearrange("t (u p e) -> t p u e", u=2, e=2)
            for q in range(4):
                blk = src[:, base + q * BLK:base + (q + 1) * BLK].bitcast(FP8)
                nc.vector.tensor_scalar(out=dst[:, 32 * q:32 * (q + 1)],
                                        in0=blk.rearrange("t (p u e) -> t p u e", u=2, e=2),
                                        scalar1=sc[:, col + q:col + q + 1], scalar2=None, op0=ALU.mult)
            st["wide", i, g] = word_blocks(wide)

        def widen_q(i, blocks):
            if not live(i):
                return
            src, base = st["qb", i]
            sc, col = st["qs", i]
            if ("wide_q", i) not in st:
                st["wide_q", i] = wtile([P, KP], BF16, "wide4", 3)
            wide = st["wide_q", i]
            st["wide", i, 4] = [wide[:].bitcast(F32)[:, u:2 * P:2] for u in range(2)]
            for q in blocks:
                blk = src[:, base + q * BLK:base + (q + 1) * BLK].bitcast(FP8)
                if q < 2 and i > 1:
                    nc.scalar.activation(out=wide[:, q * BLK:(q + 1) * BLK], in_=blk,
                                         func=ACT.Copy, scale=sc[:, col + q:col + q + 1])
                else:
                    nc.vector.tensor_scalar(out=wide[:, q * BLK:(q + 1) * BLK], in0=blk,
                                            scalar1=sc[:, col + q:col + q + 1], scalar2=None, op0=ALU.mult)

        def turn(key, i, srcs):
            if not live(i):
                return
            b = bank()
            for j, k in enumerate(srcs):
                for u in range(2):
                    nc.tensor.transpose(b[:, (2 * j + u) * P:(2 * j + u + 1) * P], st[k][u], ident[:])
            st["turned", key, i] = (b, len(srcs))

        def empty(key, i):
            if not live(i):
                return
            b, n = st["turned", key, i]
            grouped = wtile([P, n * KP], BF16, "grouped_" + key, 2)
            nc.scalar.copy(out=grouped[:].bitcast(F32).rearrange("p (j r u) -> p j r u", j=n, u=2),
                           in_=b[:, 0:n * 2 * P].rearrange("p (j u r) -> p j r u", j=n, u=2))
            st["grouped", key, i] = (grouped, n)

        def quant(key, i):
            if not live(i):
                return
            grouped, n = st["grouped", key, i]
            codes = wtile([P, n * P], U32, "codes_" + key, 2)
            scales = wtile([P, n * P], U8, "scales_" + key, 2)
            nc.vector.quantize_mx(out=codes[:].bitcast(FP8X4), scales=scales[:], in_=grouped[:])
            for j in range(n):
                st["mx", key, i, j] = (codes[:, j * P:(j + 1) * P], scales[:, j * P:(j + 1) * P])

        def product(name, w, i, j, acts, passes=None):
            if not live(i):
                return
            e = i // 2
            passes = range(len(acts)) if passes is None else passes
            b = bank() if passes[0] == 0 else st[name, i, j]
            plane = st[w, "plane", e % 2]
            for g in passes:
                codes, scales = st[acts[g]]
                col = g * F + j * N
                nc.tensor.matmul_mx(out=b[:], lhsT=codes.bitcast(FP8X4), lhsT_scale=scales,
                                    rhs=st[w, "words", e, g, j].bitcast(FP4X4),
                                    rhs_scale=plane[:, col:col + N],
                                    start=(g == 0), stop=(g == len(acts) - 1))
            st[name, i, j] = b

        def v_acts(i):
            return [("mx", "v0", i, 0), ("mx", "v0", i, 1), ("mx", "v1", i, 0), ("mx", "v1", i, 1)]

        def paired(ap):
            return ap.rearrange("t (p u e) -> t u p e", u=2, e=2)

        def plain(ap):
            return ap.rearrange("t (u p e) -> t u p e", u=2, e=2)

        def row_tile(key, i, dtype, bufs):
            if (key, i) not in st:
                st[key, i] = wtile([P, A], dtype, key, bufs)
            return st[key, i]

        def cols(j):
            return slice(0, A) if j is None else slice(j * N, (j + 1) * N)

        def sigmoid(i, j):
            if not live(i):
                return
            nc.scalar.activation(out=row_tile("mask", i, F32, 3)[:, cols(j)], in_=st["r", i, j][:], func=ACT.Sigmoid)

        def tanh(i, j):
            if not live(i):
                return
            t = wtile([P, N], F32, "tanh%d" % j, 2)
            nc.scalar.activation(out=plain(t[:]), in_=paired(st["a", i, j][:]), func=ACT.Tanh)
            st["tanh", i, j] = t

        def joint(i, j):
            if not live(i):
                return
            h = wtile([P, N], BF16, "joint%d" % j, 2)
            nc.vector.tensor_tensor(out=plain(h[:]), in0=paired(st["b", i, j][:]), in1=plain(st["tanh", i, j][:]),
                                    op=ALU.mult)
            st["h", i, j] = word_blocks(h)

        def add_bias(i, j):
            if not live(i):
                return
            nc.vector.tensor_tensor(out=row_tile("biased", i, F32, 2)[:, cols(j)], in0=st["z", i, j][:],
                                    in1=st["c_rows", i // 2][:, cols(j)], op=ALU.add)

        def apply_mask(i, j=None):
            if not live(i):
                return
            nc.vector.tensor_tensor(out=row_tile("y", i, F32, 6)[:, cols(j)], in0=st["biased", i][:, cols(j)],
                                    in1=st["mask", i][:, cols(j)], op=ALU.mult)

        def store_y(i, j=None):
            nc.sync.dma_start(out=out_0[i // 2, (i % 2) * P:(i % 2 + 1) * P, cols(j)], in_=st["y", i][:, cols(j)])

        def round_y(i):
            if not live(i):
                return
            yb = wtile([P, A], BF16, "y_bf", 2)
            nc.scalar.copy(out=plain(yb[:]), in_=paired(st["y", i][:]))
            words = yb[:].bitcast(F32)
            for j in range(2):
                st["yb", i, j] = [words[:, (2 * u + j) * P:(2 * u + j + 1) * P] for u in range(2)]

        def round_y_half(i, j):
            if not live(i):
                return
            yb = wtile([P, N], BF16, "y_bf_half", 4)
            nc.scalar.copy(out=plain(yb[:]), in_=paired(st["y", i][:, cols(j)]))
            st["yb", i, j] = word_blocks(yb)

        def store_y_scales(plane, m0, width, queues):
            rows = out_2.bitcast(I32).rearrange("g (q r) m -> r q g m", r=4)
            for r in range(4):
                queues[r % len(queues)].dma_start(out=rows[r, :, :, m0 // 4:(m0 + width) // 4],
                                  in_=plane[r:P:32, :].bitcast(I32).rearrange("q (g m) -> q g m", g=2))

        def mask_to_bf16(i, j):
            yb = wtile([P, N], BF16, "y_bf_half", 4)
            nc.vector.tensor_tensor(out=plain(yb[:]), in0=paired(st["biased", i][:, cols(j)]),
                                    in1=paired(st["mask", i][:, cols(j)]), op=ALU.mult)
            st["yb", i, j] = word_blocks(yb)

        def quant_y_half(i, j):
            grouped, n = st["grouped", "y%d" % j, i]
            codes = wtile([P, P], U32, "y_codes_half", 2)
            nc.vector.quantize_mx(out=codes[:].bitcast(FP8X4), scales=y_scales(i, j),
                                  in_=grouped[:])
            dst = out_1.rearrange("g p m t -> g p (m t)").bitcast(I32)
            nc.sync.dma_start(out=dst[j, :, i * P:(i + 1) * P], in_=codes[:].bitcast(I32))

        def quant_y(i):
            if not live(i):
                return
            grouped, n = st["grouped", "y", i]
            codes = wtile([P, 2 * P], U32, "y_codes", 6)
            for j in range(2):
                nc.vector.quantize_mx(out=codes[:, j * P:(j + 1) * P].bitcast(FP8X4), scales=y_scales(i, j),
                                      in_=grouped[:, j * KP:(j + 1) * KP])
            st["y_codes", i] = codes

        def store_codes(i):
            dst = out_1.rearrange("g p m t -> p g (m t)").bitcast(I32)
            nc.sync.dma_start(out=dst[:, :, i * P:(i + 1) * P],
                              in_=st["y_codes", i][:].bitcast(I32).rearrange("p (g m) -> p g m", g=2))
            if i == early - 1:
                store_y_scales(y_scales_early, 0, early * P, [nc.sync])

        def spread_turn(e):
            if not 0 <= e < G:
                return
            b = bank()
            cols = st["c_cols"][:].bitcast(F32)
            for j in range(4):
                nc.tensor.transpose(b[:, j * P:(j + 1) * P],
                                    cols[:, 4 * e + j:4 * e + j + 1].to_broadcast([P, P]), ident[:])
            st["c_bank", e] = b

        def spread_empty(e):
            if not 0 <= e < G:
                return
            rows = ktile([P, A], BF16, "c_rows%d" % e)
            nc.scalar.copy(out=rows[:].bitcast(F32).rearrange("t (p j) -> t p j", j=4),
                           in_=st["c_bank", e][:].rearrange("t (j p) -> t p j", j=4))
            st["c_rows", e] = rows

        def q_acts(i):
            return [("mx", "q", i, 0)]

        def h_acts(i):
            return [("mx", "h", i, 0), ("mx", "h", i, 1)]

        def turn_v(i, half):
            turn("v%d" % half, i, [("wide", i, 2 * half), ("wide", i, 2 * half + 1)])

        def turn_h(i):
            turn("h", i, [("h", i, 0), ("h", i, 1)])

        def turn_y(i):
            turn("y", i, [("yb", i, 0), ("yb", i, 1)])

        def load_pair(load, e, first):
            for w, group in ([("C", e - 1), ("U", e)] if first else [("W", e), ("R", e)]):
                load(w, group)

        load_v(0)
        load_act_scales(V_scale, "vs", 0, 2)
        load_q(0, 2)
        load_act_scales(Q_scale, "qs", 0, 2)
        load_words_half("U", 0, 0)
        load_planes("U", 0)
        load_v(1)
        load_words("R", 0)
        load_planes("R", 0)
        load_words_half("U", 0, 1)
        load_words("W", 0)
        load_planes("W", 0)
        load_v(2)
        load_act_scales(V_scale, "vs", 2, TILES - 2)
        load_q(2, 2)
        load_act_scales(Q_scale, "qs", 2, TILES - 2)
        load_c()
        load_v(3)
        load_pair(load_words, 1, True)

        for half in range(2):
            widen(0, 2 * half)
            widen(0, 2 * half + 1)
            turn_v(0, half)
            empty("v%d" % half, 0)
        widen_q(0, range(4))
        turn("q", 0, [("wide", 0, 4)])
        for w in ("R", "W", "C"):
            clear_plane(w, 1)
        quant("v0", 0)
        empty("q", 0)
        product("a", "U", 0, 0, v_acts(0), [0, 1])
        quant("v1", 0)
        product("a", "U", 0, 0, v_acts(0), [2, 3])
        quant("q", 0)
        for g in range(4):
            widen(1, g)
        widen_q(1, range(4))
        clear_plane("U", 1)
        product("r", "R", 0, 0, q_acts(0))
        product("r", "R", 0, 1, q_acts(0))
        sigmoid(0, 0)
        sigmoid(0, 1)
        turn_v(1, 0)
        turn_v(1, 1)
        turn("q", 1, [("wide", 1, 4)])
        load_pair(load_planes, 1, True)
        load_v(4)
        load_pair(load_words, 1, False)
        load_pair(load_planes, 1, False)
        load_q(4, 4)
        load_v(5)
        load_pair(load_words, 2, True)
        load_pair(load_words, 2, False)
        load_v(6)
        empty("v0", 1)
        tanh(0, 0)
        product("a", "U", 0, 1, v_acts(0))
        empty("v1", 1)
        product("b", "W", 0, 0, q_acts(0))
        product("b", "W", 0, 1, q_acts(0))
        empty("q", 1)
        widen(2, 0)
        widen(2, 1)
        widen(2, 2)
        quant("v0", 1)
        tanh(0, 1)
        quant("v1", 1)
        joint(0, 0)
        quant("q", 1)
        widen(2, 3)
        joint(0, 1)

        spread = {1: [0, 1], 2: [2], 3: [3]}
        for s in range(1, last):
            if s == 2:
                load_pair(load_planes, 2, True)
                load_pair(load_planes, 2, False)
                load_v(7)
                load_pair(load_words, 3, True)
                load_pair(load_words, 3, False)
            if s == 4:
                load_pair(load_planes, 3, True)
                load_pair(load_planes, 3, False)
                load_words("C", 3)
            if s == 5:
                load_planes("C", 3)
            n, o = s + 1, s - 2
            product("a", "U", s, 0, v_acts(s))
            add_bias(o, 1)
            apply_mask(o, 0)
            product("b", "W", s, 0, q_acts(s))
            widen_q(n, range(2))
            tanh(s, 0)
            widen(n + 1, 0)
            apply_mask(o, 1)
            product("a", "U", s, 1, v_acts(s))
            round_y_half(o, 0)
            round_y_half(o, 1)
            widen(n + 1, 1)
            widen_q(n, range(2, 4))
            joint(s, 0)
            turn_h(s - 1)
            empty("h", s - 1)
            turn_v(n, 0)
            quant_y(s - 3)
            tanh(s, 1)
            turn_v(n, 1)
            turn("q", n, [("wide", n, 4)])
            turn_y(o)
            empty("v0", n)
            for e in spread.get(s, []):
                spread_turn(e)
            widen(n + 1, 2)
            widen(n + 1, 3)
            product("b", "W", s, 1, q_acts(s))
            quant("h", s - 1)
            empty("v1", n)
            product("r", "R", s, 0, q_acts(s))
            joint(s, 1)
            empty("q", n)
            product("r", "R", s, 1, q_acts(s))
            empty("y", o)
            for e in spread.get(s, []):
                spread_empty(e)
            product("z", "C", s - 1, 0, h_acts(s - 1))
            quant("v0", n)
            quant("v1", n)
            sigmoid(s, 0)
            product("z", "C", s - 1, 1, h_acts(s - 1))
            quant("q", n)
            sigmoid(s, 1)
            add_bias(s - 1, 0)
            if s >= 4:
                for i in (range(o + 1) if s == 4 else [o]):
                    store_y(i)
                for i in (range(o) if s == 4 else [o - 1]):
                    store_codes(i)

        s = last
        h_last = [("mx", "h0", s, 0), ("mx", "h1", s, 0)]
        turn_h(s - 1)
        add_bias(s - 2, 1)
        empty("h", s - 1)
        product("a", "U", s, 0, v_acts(s))
        apply_mask(s - 2, 0)
        quant_y(s - 3)
        store_codes(s - 3)
        product("b", "W", s, 0, q_acts(s))
        tanh(s, 0)
        quant("h", s - 1)
        apply_mask(s - 2, 1)
        store_y(s - 2)
        product("a", "U", s, 1, v_acts(s))
        round_y_half(s - 2, 0)
        product("z", "C", s - 1, 0, h_acts(s - 1))
        joint(s, 0)
        tanh(s, 1)
        product("b", "W", s, 1, q_acts(s))
        product("z", "C", s - 1, 1, h_acts(s - 1))
        add_bias(s - 1, 0)
        round_y_half(s - 2, 1)
        turn("h0", s, [("h", s, 0)])
        turn_y(s - 2)
        joint(s, 1)
        empty("h0", s)
        empty("y", s - 2)
        product("r", "R", s, 0, q_acts(s))
        product("r", "R", s, 1, q_acts(s))
        add_bias(s - 1, 1)
        turn("h1", s, [("h", s, 1)])
        quant("h0", s)
        empty("h1", s)
        apply_mask(s - 1, 0)
        product("z", "C", s, 0, h_last, [0])
        product("z", "C", s, 1, h_last, [0])
        quant("h1", s)
        sigmoid(s, 0)
        product("z", "C", s, 0, h_last, [1])
        product("z", "C", s, 1, h_last, [1])
        apply_mask(s - 1, 1)
        sigmoid(s, 1)
        store_y(s - 1)
        quant_y(s - 2)
        store_codes(s - 2)
        round_y_half(s - 1, 0)
        add_bias(s, 0)
        round_y_half(s - 1, 1)
        add_bias(s, 1)
        turn_y(s - 1)
        apply_mask(s, 0)
        store_y(s, 0)
        empty("y", s - 1)
        mask_to_bf16(s, 1)
        round_y_half(s, 0)
        apply_mask(s, 1)
        store_y(s, 1)
        turn("y1", s, [("yb", s, 1)])
        turn("y0", s, [("yb", s, 0)])
        empty("y1", s)
        empty("y0", s)
        quant_y(s - 1)
        store_codes(s - 1)
        quant_y_half(s, 1)
        quant_y_half(s, 0)
        store_y_scales(y_scales_last, early * P, 2 * P, [nc.sync])
